import numpy as np
import ml_dtypes


def mxq(x, axis, fmt="e4m3"):
    dtype, down = {"e4m3": (ml_dtypes.float8_e4m3fn, 7), "e5m2": (ml_dtypes.float8_e5m2, 14)}[fmt]
    v = np.moveaxis(np.asarray(x, np.float32).astype(ml_dtypes.bfloat16).astype(np.float64), axis, -1)
    blocks = v.reshape(v.shape[:-1] + (-1, 32))
    amax = np.abs(blocks).max(-1, keepdims=True)
    byte = np.maximum(np.where(amax > 0, np.frexp(amax)[1] - 1 + 127, 0) - down, 1)
    scale = np.exp2(byte - 127.0)
    codes = (blocks / scale).astype(np.float32).astype(dtype).astype(np.float64)
    return np.moveaxis((codes * scale).reshape(v.shape), -1, axis)


WIDE = False


def mx_kscale(k):
    if not WIDE:
        return np.ones(k)
    levels = np.array([30, -30])
    if k % 512:
        return np.exp2(np.random.permutation(np.resize(levels, k // 32))).repeat(32)
    a = np.empty((k // 512, 16))
    for p in range(k // 512):
        a[p, :8] = np.random.permutation(np.resize(levels, 8))
        for g in range(8):
            far = levels[np.abs(levels - a[p, g]) >= 10]
            a[p, g + 8] = far[np.random.randint(len(far))]
    return np.exp2(a.ravel()).repeat(32)


def f64(x):
    return np.asarray(x).astype(np.float64)


def striped(idx):
    return np.tile(np.asarray(idx).reshape(-1, 16).T, (8, 1)).astype(np.uint16)


def unstriped(offs):
    return offs[:16].T.reshape(-1).astype(np.int64)


E2M1 = np.array([0.0, 0.5, 1.0, 1.5, 2.0, 3.0, 4.0, 6.0, -0.0, -0.5, -1.0, -1.5, -2.0, -3.0, -4.0, -6.0])


def pack_weight(w, fmt):
    k, n = w.shape
    w = f64(np.asarray(w, np.float32).astype(ml_dtypes.bfloat16)).reshape(k // 32, 32, n)
    amax = np.abs(w).max(1)
    if fmt == "e4m3":
        byte = np.frexp(amax)[1] - 1 + 127 - 7
    else:
        mant, ex = np.frexp(amax / 6.0)
        byte = np.where(mant > 0.5, ex, ex - 1) + 127
    byte = np.clip(np.where(amax > 0, byte, 1), 1, 254)
    scaled = (w * np.exp2(127.0 - byte)[:, None, :]).reshape(k, n).astype(np.float32)
    by_word = np.ascontiguousarray(scaled.reshape(k // 512, 128, 4, n).transpose(0, 1, 3, 2))
    if fmt == "e4m3":
        words = by_word.astype(ml_dtypes.float8_e4m3fn).view(np.uint8)
    else:
        c = by_word.astype(ml_dtypes.float4_e2m1fn).view(np.uint8) & 0xF
        words = (c[..., 0::2] | (c[..., 1::2] << 4)).reshape(k // 512, 128, 2 * n)
    return np.ascontiguousarray(words), np.ascontiguousarray(byte.astype(np.uint8).reshape(k // 512, 16, n))


def unpack_weight(words, scales, fmt):
    g, _, n = scales.shape
    words = np.ascontiguousarray(words).reshape(g, 128, n, -1)
    if fmt == "e4m3":
        vals = words.view(ml_dtypes.float8_e4m3fn).astype(np.float64)
    else:
        nib = np.empty((g, 128, n, 4), np.uint8)
        nib[..., 0::2] = words & 0xF
        nib[..., 1::2] = words >> 4
        vals = E2M1[nib]
    vals = vals * np.repeat(np.exp2(scales.astype(np.float64) - 127.0), 8, axis=1)[..., None]
    return vals.transpose(0, 1, 3, 2).reshape(g * 512, n)


def sgn(shape):
    return np.random.uniform(0.5, 2.0, shape) * np.where(np.random.standard_normal(shape) < 0, -1.0, 1.0)


K, T, J, R, I, O, N, E = 512, 1024, 256, 512, 256, 128, 256, 1024


def setup_inputs():
    n = np.random.standard_normal
    idx = np.random.permutation(T)[:J]
    idx2 = np.random.permutation(J)[:I]
    idx3 = np.random.permutation(T)[:O]
    idx4 = np.random.permutation(E)[:O]
    fk = mx_kscale(K)
    fr = mx_kscale(R)
    xtp = pack_weight(n((K, T)) / fk[:, None], "e2m1")
    wp = pack_weight(n((K, R)) * 1 / np.sqrt(K) * fk[:, None] * fr, "e4m3")
    wbp = pack_weight(n((R, N)) * 1 / np.sqrt(R) / fr[:, None], "e2m1")
    wsp = pack_weight(n((K, N)) * 1 / np.sqrt(K) * fk[:, None], "e4m3")
    return {
        "xt_words": xtp[0],
        "xt_scales": xtp[1],
        "w_words": wp[0],
        "w_scales": wp[1],
        "sa": (sgn((R, 1))).astype(np.float32),
        "wb_words": wbp[0],
        "wb_scales": wbp[1],
        "ws_words": wsp[0],
        "ws_scales": wsp[1],
        "tz": (n((N, E))).astype(np.float32),
        "offs": striped(idx),
        "offs2": striped(idx2),
        "offs3": striped(idx3),
        "offs4": striped(idx4),
    }


def reference(xt_words, xt_scales, w_words, w_scales, sa, wb_words, wb_scales, ws_words, ws_scales, tz, offs, offs2, offs3, offs4):
    idx = unstriped(offs)
    idx2 = unstriped(offs2)
    idx3 = unstriped(offs3)
    idx4 = unstriped(offs4)
    xtu = unpack_weight(xt_words, xt_scales, "e2m1")
    wu = unpack_weight(w_words, w_scales, "e4m3")
    wbu = unpack_weight(wb_words, wb_scales, "e2m1")
    wsu = unpack_weight(ws_words, ws_scales, "e4m3")
    xtidxg = xtu[:, idx]
    a = wu.T @ xtidxg
    h1 = a[:, idx2] * f64(sa)
    hid = h1.reshape(R, O, I // O).max(axis=2)
    hidq = mxq(hid, 0, "e5m2")
    xtidx3g = xtu[:, idx3]
    p = wbu.T @ hidq + wsu.T @ xtidx3g
    y = p + f64(tz)[:, idx4]
    return y

@@ -1,0 +1,182 @@
+from contextlib import ExitStack
+
+import concourse.mybir as mybir
+
+K, T, J, R, I, O, N, E = 512, 1024, 256, 512, 256, 128, 256, 1024
+FLOPS = 2 * K * R * J + 2 * R * N * O + 2 * K * N * O
+
+F32 = mybir.dt.float32
+BF16 = mybir.dt.bfloat16
+I32 = mybir.dt.int32
+U32 = mybir.dt.uint32
+U16 = mybir.dt.uint16
+U8 = mybir.dt.uint8
+E4M3X4 = mybir.dt.float8_e4m3fn_x4
+E5M2X4 = mybir.dt.float8_e5m2_x4
+E2M1X4 = mybir.dt.float4_e2m1fn_x4
+COPY = mybir.ActivationFunctionType.Copy
+MAX = mybir.AluOpType.max
+ADD = mybir.AluOpType.add
+
+P = 128
+PACK = 4
+HALF = I // 2
+
+
+def load_scale_rows(queue, tile_words, scales):
+    rows = scales[0].bitcast(I32).rearrange("(h q r) c -> q r h c", h=2, q=2)
+    for q in range(2):
+        queue.dma_start(out=tile_words[32 * q : 32 * q + 4], in_=rows[q])
+
+
+def spread_scale_rows(nc, tile):
+    words = tile[:].bitcast(I32)
+    nc.vector.tensor_copy(out=words[64:128, 0, :], in_=words[0:64, 1, :])
+
+
+def tile_list_pooledpicks_solo_further_tabled_kernel(
+    tc, xt_words, xt_scales, w_words, w_scales, sa, wb_words, wb_scales, ws_words, ws_scales, tz,
+    offs, offs2, offs3, offs4, out,
+):
+    nc = tc.nc
+    with ExitStack() as ctx:
+        keep = ctx.enter_context(tc.tile_pool(name="keep", bufs=1))
+        psum = ctx.enter_context(tc.psum_pool(name="psum", bufs=1))
+
+        list1 = keep.tile([P, J // 16], U16, name="list1")
+        list2 = keep.tile([P, I // 16], U16, name="list2")
+        list3 = keep.tile([P, O // 16], U16, name="list3")
+        list4 = keep.tile([P, O // 16], U16, name="list4")
+        xt_w = keep.tile([P, T], U16, name="xt_w", align_bytes=64)
+        xt_stage = keep.tile([P, 2, T], U8, name="xt_stage", align_bytes=64)
+        xt_s = keep.tile([P, T], U8, name="xt_s", align_bytes=64)
+        w_w = keep.tile([P, R], U32, name="w_w", align_bytes=64)
+        w_s = keep.tile([P, 2, R], U8, name="w_s", align_bytes=64)
+        late_s = keep.tile([P, 2, 2 * N], U8, name="late_s", align_bytes=64)
+        ws_w = keep.tile([P, N], U32, name="ws_w", align_bytes=64)
+        wb_w = keep.tile([P, 2 * N], U8, name="wb_w", align_bytes=64)
+        sa_t = keep.tile([P, PACK], F32, name="sa_t")
+        tz_t = keep.tile([P, 2, E], F32, name="tz_t")
+
+        for tile in (xt_stage, w_s, late_s):
+            nc.vector.memset(tile[:].bitcast(I32), 0)
+
+        nc.sync.dma_start(out=xt_w[:].bitcast(I32), in_=xt_words[0].bitcast(I32))
+        nc.sync.dma_start(list1[:], offs)
+        nc.sync.dma_start(out=w_w[:].bitcast(I32), in_=w_words[0].rearrange("p n t -> p (n t)").bitcast(I32))
+        load_scale_rows(nc.scalar, xt_stage[:].bitcast(I32), xt_scales)
+        load_scale_rows(nc.scalar, w_s[:].bitcast(I32), w_scales)
+        nc.sync.dma_start(list2[:], offs2)
+        nc.gpsimd.dma_start(out=sa_t[:], in_=sa.rearrange("(p t) o -> p (t o)", t=PACK))
+        late_words = late_s[:].bitcast(I32)
+        load_scale_rows(nc.gpsimd, late_words[:, :, N // 4 : N // 2], wb_scales)
+        load_scale_rows(nc.sync, late_words[:, :, 0 : N // 4], ws_scales)
+        nc.sync.dma_start(list3[:], offs3)
+        nc.sync.dma_start(out=ws_w[:].bitcast(I32), in_=ws_words[0].rearrange("p n t -> p (n t)").bitcast(I32))
+        nc.sync.dma_start(out=wb_w[:].bitcast(I32), in_=wb_words[0].bitcast(I32))
+        nc.sync.dma_start(list4[:], offs4)
+        nc.sync.dma_start(out=tz_t[:], in_=tz.rearrange("(b p) e -> p b e", p=P))
+
+        for h in range(2):
+            nc.vector.tensor_copy(
+                out=xt_s[64 * h : 64 * (h + 1), :].bitcast(I32), in_=xt_stage[0:64, h, :].bitcast(I32)
+            )
+        spread_scale_rows(nc, w_s)
+        w_sp = keep.tile([P, PACK, P], U8, name="w_sp", align_bytes=64)
+        nc.vector.tensor_copy(out=w_sp[:], in_=w_s[:, 0, :].rearrange("p (m t) -> p t m", t=PACK))
+        w_wp = [keep.tile([P, 2, P], U32, name=f"w_wp{u}", align_bytes=64) for u in range(2)]
+        w_by_t = w_w[:].rearrange("p (c i t) -> p c t i", i=4, t=PACK)
+        for u in range(2):
+            nc.scalar.copy(
+                out=w_wp[u][:].rearrange("p t (c i) -> p c t i", i=4), in_=w_by_t[:, :, 2 * u : 2 * u + 2, :]
+            )
+
+        x1_s = keep.tile([P, J], U8, name="x1_s", align_bytes=64)
+        x1_w = keep.tile([P, J], U16, name="x1_w", align_bytes=64)
+        nc.vector.tensor_copy(x1_s[:], xt_s[:].indirect(list1[:]))
+        nc.vector.tensor_copy(x1_w[:], xt_w[:].indirect(list1[:]))
+
+        a_t = []
+        for t in range(PACK):
+            acc = psum.tile([P, J], F32, name=f"acc{t}")
+            nc.tensor.matmul_mx(
+                out=acc[:],
+                lhsT=w_wp[t // 2][:, t % 2, :].bitcast(E4M3X4),
+                lhsT_scale=w_sp[:, t, :],
+                rhs=x1_w[:].bitcast(E2M1X4),
+                rhs_scale=x1_s[:],
+                start=True,
+                stop=True,
+            )
+            rows = keep.tile([P, J], F32, name=f"a{t}")
+            nc.vector.tensor_copy(out=rows[:], in_=acc[:])
+            a_t.append(rows)
+
+        hid = keep.tile([P, O, PACK], BF16, name="hid", align_bytes=64)
+        hid_w = keep.tile([P, O], U32, name="hid_w", align_bytes=64)
+        hid_s = keep.tile([P, O], U8, name="hid_s", align_bytes=64)
+
+        def pick(dst, t, h):
+            nc.scalar.activation(
+                out=dst,
+                in_=a_t[t][:].indirect(list2[:, 8 * h : 8 * h + 8]),
+                func=COPY,
+                scale=sa_t[:, t : t + 1],
+            )
+
+        def pool_pairs(picks, pools, t0):
+            pairs = picks.rearrange("p (t o e) -> p e o t", t=2, e=2)
+            nc.vector.tensor_tensor(out=hid[:, pools, t0 : t0 + 2], in0=pairs[:, 0], in1=pairs[:, 1], op=MAX)
+
+        h1_lo = keep.tile([P, 2 * I], F32, name="h1_lo")
+        for t in range(2):
+            for h in range(2):
+                pick(h1_lo[:, t * I + h * HALF : t * I + (h + 1) * HALF], t, h)
+        pool_pairs(h1_lo[:], slice(0, O), 0)
+
+        x3_s = keep.tile([P, O], U8, name="x3_s", align_bytes=64)
+        x3_w = keep.tile([P, O], U16, name="x3_w", align_bytes=64)
+        nc.vector.tensor_copy(x3_s[:], xt_s[:].indirect(list3[:]))
+        nc.vector.tensor_copy(x3_w[:], xt_w[:].indirect(list3[:]))
+        spread_scale_rows(nc, late_s)
+        res = [psum.tile([P, O], F32, name=f"res{b}") for b in range(2)]
+        for b in range(2):
+            nc.tensor.matmul_mx(
+                out=res[b][:],
+                lhsT=ws_w[:, b * P : (b + 1) * P].bitcast(E4M3X4),
+                lhsT_scale=late_s[:, 0, b * P : (b + 1) * P],
+                rhs=x3_w[:].bitcast(E2M1X4),
+                rhs_scale=x3_s[:],
+                start=True,
+                stop=False,
+            )
+
+        for h in range(2):
+            h1_hi = keep.tile([P, 2 * HALF], F32, name=f"h1_hi{h}")
+            for t in range(2, 4):
+                pick(h1_hi[:, (t - 2) * HALF : (t - 1) * HALF], t, h)
+            pools = slice(h * O // 2, (h + 1) * O // 2)
+            pool_pairs(h1_hi[:], pools, 2)
+            nc.vector.quantize_mx(
+                out=hid_w[:, pools].bitcast(E5M2X4),
+                scales=hid_s[:, pools],
+                in_=hid[:, pools, :].rearrange("p o t -> p (o t)"),
+            )
+
+        tz_g = keep.tile([P, 2, O], F32, name="tz_g", tag="a3")
+        for b in range(2):
+            nc.scalar.activation(out=tz_g[:, b, :], in_=tz_t[:, b, :].indirect(list4[:]), func=COPY)
+
+        for b in range(2):
+            nc.tensor.matmul_mx(
+                out=res[b][:],
+                lhsT=wb_w[:, 2 * b * P : 2 * (b + 1) * P].bitcast(E2M1X4),
+                lhsT_scale=late_s[:, 0, N + b * P : N + (b + 1) * P],
+                rhs=hid_w[:].bitcast(E5M2X4),
+                rhs_scale=hid_s[:],
+                start=False,
+                stop=True,
+            )
+            y = keep.tile([P, O], F32, name=f"y{b}")
+            nc.vector.tensor_tensor(out=y[:], in0=res[b][:], in1=tz_g[:, b, :], op=ADD)
+            (nc.sync if b == 0 else nc.scalar).dma_start(out=out[b * P : (b + 1) * P, :], in_=y[:])

@@ -23,15 +23,9 @@ PACK = 4
 HALF = I // 2
 
 
-def load_scale_rows(queue, tile_words, scales):
+def load_scale_rows(queue, tile_words, scales, q, first):
     rows = scales[0].bitcast(I32).rearrange("(h q r) c -> q r h c", h=2, q=2)
-    for q in range(2):
-        queue.dma_start(out=tile_words[32 * q : 32 * q + 4], in_=rows[q])
-
-
-def spread_scale_rows(nc, tile):
-    words = tile[:].bitcast(I32)
-    nc.vector.tensor_copy(out=words[64:128, 0, :], in_=words[0:64, 1, :])
+    queue.dma_start(out=tile_words[first + 32 * q : first + 32 * q + 4], in_=rows[q])
 
 
 def tile_list_pooledpicks_solo_further_tabled_kernel(
@@ -48,42 +42,54 @@ def tile_list_pooledpicks_solo_further_tabled_kernel(
         list3 = keep.tile([P, O // 16], U16, name="list3")
         list4 = keep.tile([P, O // 16], U16, name="list4")
         xt_w = keep.tile([P, T], U16, name="xt_w", align_bytes=64)
-        xt_stage = keep.tile([P, 2, T], U8, name="xt_stage", align_bytes=64)
         xt_s = keep.tile([P, T], U8, name="xt_s", align_bytes=64)
         w_w = keep.tile([P, R], U32, name="w_w", align_bytes=64)
-        w_s = keep.tile([P, 2, R], U8, name="w_s", align_bytes=64)
+        w_stage = keep.tile([4, 4, R // 4], I32, name="w_stage", align_bytes=64)
+        w_s = keep.tile([P, R], U8, name="w_s", align_bytes=64)
         late_s = keep.tile([P, 2, 2 * N], U8, name="late_s", align_bytes=64)
         ws_w = keep.tile([P, N], U32, name="ws_w", align_bytes=64)
         wb_w = keep.tile([P, 2 * N], U8, name="wb_w", align_bytes=64)
         sa_t = keep.tile([P, PACK], F32, name="sa_t")
         tz_t = keep.tile([P, 2, E], F32, name="tz_t")
 
-        for tile in (xt_stage, w_s, late_s):
-            nc.vector.memset(tile[:].bitcast(I32), 0)
+        warm = keep.tile([P, 2], F32, name="warm")
+        nc.vector.memset(xt_s[:].bitcast(I32), 0)
+        nc.vector.memset(warm[:, 0:1], 0.0)
+        for tile in (w_s, late_s):
+            nc.gpsimd.memset(tile[:].bitcast(I32), 0)
 
+        xt_s_words = xt_s[:].bitcast(I32)
+        xt_rows = xt_scales[0].bitcast(I32)
+        w_s_words = w_s[:].bitcast(I32)
+        ws_s_words = late_s[:].bitcast(I32)[:, :, 0 : N // 4]
+        wb_s_words = late_s[:].bitcast(I32)[:, :, N // 4 : N // 2]
+        nc.sync.dma_start(out=w_stage[:], in_=w_scales[0].bitcast(I32).rearrange("(q r) c -> r q c", q=4))
         nc.sync.dma_start(out=xt_w[:].bitcast(I32), in_=xt_words[0].bitcast(I32))
         nc.sync.dma_start(list1[:], offs)
         nc.sync.dma_start(out=w_w[:].bitcast(I32), in_=w_words[0].rearrange("p n t -> p (n t)").bitcast(I32))
-        load_scale_rows(nc.scalar, xt_stage[:].bitcast(I32), xt_scales)
-        load_scale_rows(nc.scalar, w_s[:].bitcast(I32), w_scales)
-        nc.sync.dma_start(list2[:], offs2)
-        nc.gpsimd.dma_start(out=sa_t[:], in_=sa.rearrange("(p t) o -> p (t o)", t=PACK))
-        late_words = late_s[:].bitcast(I32)
-        load_scale_rows(nc.gpsimd, late_words[:, :, N // 4 : N // 2], wb_scales)
-        load_scale_rows(nc.sync, late_words[:, :, 0 : N // 4], ws_scales)
+        for q in range(4):
+            nc.scalar.dma_start(out=xt_s_words[32 * q : 32 * q + 4, :], in_=xt_rows[4 * q : 4 * q + 4, :])
+        nc.scalar.activation(out=warm[:, 1:2], in_=warm[:, 0:1], func=COPY)
         nc.sync.dma_start(list3[:], offs3)
+        nc.sync.dma_start(list2[:], offs2)
+        nc.sync.dma_start(out=sa_t[:], in_=sa.rearrange("(p t) o -> p (t o)", t=PACK))
+        for q in range(2):
+            load_scale_rows(nc.scalar, wb_s_words, wb_scales, q, 64)
+        for q in range(2):
+            load_scale_rows(nc.sync, ws_s_words, ws_scales, q, 64)
+        nc.sync.dma_start(out=tz_t[:], in_=tz.rearrange("(b p) e -> p b e", p=P))
         nc.sync.dma_start(out=ws_w[:].bitcast(I32), in_=ws_words[0].rearrange("p n t -> p (n t)").bitcast(I32))
         nc.sync.dma_start(out=wb_w[:].bitcast(I32), in_=wb_words[0].bitcast(I32))
         nc.sync.dma_start(list4[:], offs4)
-        nc.sync.dma_start(out=tz_t[:], in_=tz.rearrange("(b p) e -> p b e", p=P))
 
-        for h in range(2):
-            nc.vector.tensor_copy(
-                out=xt_s[64 * h : 64 * (h + 1), :].bitcast(I32), in_=xt_stage[0:64, h, :].bitcast(I32)
-            )
-        spread_scale_rows(nc, w_s)
-        w_sp = keep.tile([P, PACK, P], U8, name="w_sp", align_bytes=64)
-        nc.vector.tensor_copy(out=w_sp[:], in_=w_s[:, 0, :].rearrange("p (m t) -> p t m", t=PACK))
+        for q in range(4):
+            nc.vector.tensor_copy(out=w_s_words[32 * q : 32 * q + 4, :], in_=w_stage[:, q, :])
+        w_s_by_t = w_s[:].rearrange("p (m t) -> p t m", t=PACK)
+        w_sp0 = keep.tile([P, P], U8, name="w_sp0", align_bytes=64)
+        w_sp123 = keep.tile([P, PACK - 1, P], U8, name="w_sp123", align_bytes=64)
+        nc.vector.tensor_copy(out=w_sp0[:], in_=w_s_by_t[:, 0, :])
+        nc.gpsimd.tensor_copy(out=w_sp123[:], in_=w_s_by_t[:, 1:PACK, :])
+        w_sp = [w_sp0[:]] + [w_sp123[:, t, :] for t in range(PACK - 1)]
         w_wp = [keep.tile([P, 2, P], U32, name=f"w_wp{u}", align_bytes=64) for u in range(2)]
         w_by_t = w_w[:].rearrange("p (c i t) -> p c t i", i=4, t=PACK)
         for u in range(2):
@@ -93,33 +99,46 @@ def tile_list_pooledpicks_solo_further_tabled_kernel(
 
         x1_s = keep.tile([P, J], U8, name="x1_s", align_bytes=64)
         x1_w = keep.tile([P, J], U16, name="x1_w", align_bytes=64)
-        nc.vector.tensor_copy(x1_s[:], xt_s[:].indirect(list1[:]))
         nc.vector.tensor_copy(x1_w[:], xt_w[:].indirect(list1[:]))
+        for h in range(2):
+            nc.vector.tensor_copy(x1_s[:, h * P : (h + 1) * P], xt_s[:].indirect(list1[:, 8 * h : 8 * h + 8]))
 
-        a_t = []
-        for t in range(PACK):
-            acc = psum.tile([P, J], F32, name=f"acc{t}")
+        def first_stage(t, cols, name):
+            acc = psum.tile([P, cols.stop - cols.start], F32, name=name)
             nc.tensor.matmul_mx(
                 out=acc[:],
                 lhsT=w_wp[t // 2][:, t % 2, :].bitcast(E4M3X4),
-                lhsT_scale=w_sp[:, t, :],
-                rhs=x1_w[:].bitcast(E2M1X4),
-                rhs_scale=x1_s[:],
+                lhsT_scale=w_sp[t],
+                rhs=x1_w[:, cols].bitcast(E2M1X4),
+                rhs_scale=x1_s[:, cols],
                 start=True,
                 stop=True,
             )
-            rows = keep.tile([P, J], F32, name=f"a{t}")
-            nc.vector.tensor_copy(out=rows[:], in_=acc[:])
-            a_t.append(rows)
+            return acc
 
+        a_t = [keep.tile([P, 2 * J if t < 2 else J], F32, name=f"a{t}") for t in range(PACK)]
+        nc.scalar.copy(out=a_t[0][:, 0:P], in_=first_stage(0, slice(0, P), "acc0_lo")[:])
+        nc.vector.tensor_copy(out=a_t[0][:, P:J], in_=first_stage(0, slice(P, J), "acc0_hi")[:])
+        for t in range(1, PACK):
+            nc.vector.tensor_copy(out=a_t[t][:, 0:J], in_=first_stage(t, slice(0, J), f"acc{t}")[:])
+
+        x3_s = keep.tile([P, O], U8, name="x3_s", align_bytes=64)
+        x3_w = keep.tile([P, O], U16, name="x3_w", align_bytes=64)
+        nc.vector.tensor_copy(x3_s[:], xt_s[:].indirect(list3[:]))
+        nc.vector.tensor_copy(x3_w[:], xt_w[:].indirect(list3[:]))
+        late_p = keep.tile([P, 2 * N], U8, name="late_p", tag="w_wp1", align_bytes=64)
+        for h in range(2):
+            nc.vector.tensor_copy(
+                out=late_p[64 * h : 64 * (h + 1), :].bitcast(I32), in_=late_s[64:128, h, :].bitcast(I32)
+            )
         hid = keep.tile([P, O, PACK], BF16, name="hid", align_bytes=64)
         hid_w = keep.tile([P, O], U32, name="hid_w", align_bytes=64)
         hid_s = keep.tile([P, O], U8, name="hid_s", align_bytes=64)
 
-        def pick(dst, t, h):
+        def pick(dst, t, cols):
             nc.scalar.activation(
                 out=dst,
-                in_=a_t[t][:].indirect(list2[:, 8 * h : 8 * h + 8]),
+                in_=a_t[t][:].indirect(list2[:, cols]),
                 func=COPY,
                 scale=sa_t[:, t : t + 1],
             )
@@ -130,21 +149,15 @@ def tile_list_pooledpicks_solo_further_tabled_kernel(
 
         h1_lo = keep.tile([P, 2 * I], F32, name="h1_lo")
         for t in range(2):
-            for h in range(2):
-                pick(h1_lo[:, t * I + h * HALF : t * I + (h + 1) * HALF], t, h)
+            pick(h1_lo[:, t * I : (t + 1) * I], t, slice(0, 16))
         pool_pairs(h1_lo[:], slice(0, O), 0)
 
-        x3_s = keep.tile([P, O], U8, name="x3_s", align_bytes=64)
-        x3_w = keep.tile([P, O], U16, name="x3_w", align_bytes=64)
-        nc.vector.tensor_copy(x3_s[:], xt_s[:].indirect(list3[:]))
-        nc.vector.tensor_copy(x3_w[:], xt_w[:].indirect(list3[:]))
-        spread_scale_rows(nc, late_s)
         res = [psum.tile([P, O], F32, name=f"res{b}") for b in range(2)]
         for b in range(2):
             nc.tensor.matmul_mx(
                 out=res[b][:],
                 lhsT=ws_w[:, b * P : (b + 1) * P].bitcast(E4M3X4),
-                lhsT_scale=late_s[:, 0, b * P : (b + 1) * P],
+                lhsT_scale=late_p[:, b * P : (b + 1) * P],
                 rhs=x3_w[:].bitcast(E2M1X4),
                 rhs_scale=x3_s[:],
                 start=True,
@@ -154,7 +167,7 @@ def tile_list_pooledpicks_solo_further_tabled_kernel(
         for h in range(2):
             h1_hi = keep.tile([P, 2 * HALF], F32, name=f"h1_hi{h}")
             for t in range(2, 4):
-                pick(h1_hi[:, (t - 2) * HALF : (t - 1) * HALF], t, h)
+                pick(h1_hi[:, (t - 2) * HALF : (t - 1) * HALF], t, slice(8 * h, 8 * h + 8))
             pools = slice(h * O // 2, (h + 1) * O // 2)
             pool_pairs(h1_hi[:], pools, 2)
             nc.vector.quantize_mx(
@@ -171,7 +184,7 @@ def tile_list_pooledpicks_solo_further_tabled_kernel(
             nc.tensor.matmul_mx(
                 out=res[b][:],
                 lhsT=wb_w[:, 2 * b * P : 2 * (b + 1) * P].bitcast(E2M1X4),
-                lhsT_scale=late_s[:, 0, N + b * P : N + (b + 1) * P],
+                lhsT_scale=late_p[:, N + b * P : N + (b + 1) * P],
                 rhs=hid_w[:].bitcast(E5M2X4),
                 rhs_scale=hid_s[:],
                 start=False,

@@ -23,9 +23,10 @@ PACK = 4
 HALF = I // 2
 
 
-def load_scale_rows(queue, tile_words, scales, q, first):
-    rows = scales[0].bitcast(I32).rearrange("(h q r) c -> q r h c", h=2, q=2)
-    queue.dma_start(out=tile_words[first + 32 * q : first + 32 * q + 4], in_=rows[q])
+def load_scale_rows(queue, plane, scales, q):
+    queue.dma_start(
+        out=plane[32 * q : 32 * q + 4, :].bitcast(I32), in_=scales[0].bitcast(I32)[4 * q : 4 * q + 4, :]
+    )
 
 
 def tile_list_pooledpicks_solo_further_tabled_kernel(
@@ -46,50 +47,41 @@ def tile_list_pooledpicks_solo_further_tabled_kernel(
         w_w = keep.tile([P, R], U32, name="w_w", align_bytes=64)
         w_stage = keep.tile([4, 4, R // 4], I32, name="w_stage", align_bytes=64)
         w_s = keep.tile([P, R], U8, name="w_s", align_bytes=64)
-        late_s = keep.tile([P, 2, 2 * N], U8, name="late_s", align_bytes=64)
+        ws_s = keep.tile([P, N], U8, name="ws_s", align_bytes=64)
+        wb_s = keep.tile([P, N], U8, name="wb_s", align_bytes=64)
         ws_w = keep.tile([P, N], U32, name="ws_w", align_bytes=64)
         wb_w = keep.tile([P, 2 * N], U8, name="wb_w", align_bytes=64)
         sa_t = keep.tile([P, PACK], F32, name="sa_t")
         tz_t = keep.tile([P, 2, E], F32, name="tz_t")
 
-        warm = keep.tile([P, 2], F32, name="warm")
         nc.vector.memset(xt_s[:].bitcast(I32), 0)
-        nc.vector.memset(warm[:, 0:1], 0.0)
-        for tile in (w_s, late_s):
-            nc.gpsimd.memset(tile[:].bitcast(I32), 0)
+        nc.vector.memset(w_s[:].bitcast(I32), 0)
 
-        xt_s_words = xt_s[:].bitcast(I32)
-        xt_rows = xt_scales[0].bitcast(I32)
         w_s_words = w_s[:].bitcast(I32)
-        ws_s_words = late_s[:].bitcast(I32)[:, :, 0 : N // 4]
-        wb_s_words = late_s[:].bitcast(I32)[:, :, N // 4 : N // 2]
         nc.sync.dma_start(out=w_stage[:], in_=w_scales[0].bitcast(I32).rearrange("(q r) c -> r q c", q=4))
         nc.sync.dma_start(out=xt_w[:].bitcast(I32), in_=xt_words[0].bitcast(I32))
         nc.sync.dma_start(list1[:], offs)
         nc.sync.dma_start(out=w_w[:].bitcast(I32), in_=w_words[0].rearrange("p n t -> p (n t)").bitcast(I32))
         for q in range(4):
-            nc.scalar.dma_start(out=xt_s_words[32 * q : 32 * q + 4, :], in_=xt_rows[4 * q : 4 * q + 4, :])
-        nc.scalar.activation(out=warm[:, 1:2], in_=warm[:, 0:1], func=COPY)
-        nc.sync.dma_start(list3[:], offs3)
+            load_scale_rows(nc.sync, xt_s, xt_scales, q)
         nc.sync.dma_start(list2[:], offs2)
         nc.sync.dma_start(out=sa_t[:], in_=sa.rearrange("(p t) o -> p (t o)", t=PACK))
-        for q in range(2):
-            load_scale_rows(nc.scalar, wb_s_words, wb_scales, q, 64)
-        for q in range(2):
-            load_scale_rows(nc.sync, ws_s_words, ws_scales, q, 64)
+        nc.sync.dma_start(list3[:], offs3)
+        nc.sync.dma_start(list4[:], offs4)
+        for q in range(3):
+            load_scale_rows(nc.sync, ws_s, ws_scales, q)
         nc.sync.dma_start(out=tz_t[:], in_=tz.rearrange("(b p) e -> p b e", p=P))
+        load_scale_rows(nc.sync, ws_s, ws_scales, 3)
         nc.sync.dma_start(out=ws_w[:].bitcast(I32), in_=ws_words[0].rearrange("p n t -> p (n t)").bitcast(I32))
         nc.sync.dma_start(out=wb_w[:].bitcast(I32), in_=wb_words[0].bitcast(I32))
-        nc.sync.dma_start(list4[:], offs4)
+        for q in range(4):
+            load_scale_rows(nc.sync, wb_s, wb_scales, q)
 
         for q in range(4):
             nc.vector.tensor_copy(out=w_s_words[32 * q : 32 * q + 4, :], in_=w_stage[:, q, :])
         w_s_by_t = w_s[:].rearrange("p (m t) -> p t m", t=PACK)
-        w_sp0 = keep.tile([P, P], U8, name="w_sp0", align_bytes=64)
-        w_sp123 = keep.tile([P, PACK - 1, P], U8, name="w_sp123", align_bytes=64)
-        nc.vector.tensor_copy(out=w_sp0[:], in_=w_s_by_t[:, 0, :])
-        nc.gpsimd.tensor_copy(out=w_sp123[:], in_=w_s_by_t[:, 1:PACK, :])
-        w_sp = [w_sp0[:]] + [w_sp123[:, t, :] for t in range(PACK - 1)]
+        w_sp = keep.tile([P, PACK, P], U8, name="w_sp", align_bytes=64)
+        nc.vector.tensor_copy(out=w_sp[:], in_=w_s_by_t)
         w_wp = [keep.tile([P, 2, P], U32, name=f"w_wp{u}", align_bytes=64) for u in range(2)]
         w_by_t = w_w[:].rearrange("p (c i t) -> p c t i", i=4, t=PACK)
         for u in range(2):
@@ -108,7 +100,7 @@ def tile_list_pooledpicks_solo_further_tabled_kernel(
             nc.tensor.matmul_mx(
                 out=acc[:],
                 lhsT=w_wp[t // 2][:, t % 2, :].bitcast(E4M3X4),
-                lhsT_scale=w_sp[t],
+                lhsT_scale=w_sp[:, t, :],
                 rhs=x1_w[:, cols].bitcast(E2M1X4),
                 rhs_scale=x1_s[:, cols],
                 start=True,
@@ -118,19 +110,14 @@ def tile_list_pooledpicks_solo_further_tabled_kernel(
 
         a_t = [keep.tile([P, 2 * J if t < 2 else J], F32, name=f"a{t}") for t in range(PACK)]
         nc.scalar.copy(out=a_t[0][:, 0:P], in_=first_stage(0, slice(0, P), "acc0_lo")[:])
-        nc.vector.tensor_copy(out=a_t[0][:, P:J], in_=first_stage(0, slice(P, J), "acc0_hi")[:])
+        nc.scalar.copy(out=a_t[0][:, P:J], in_=first_stage(0, slice(P, J), "acc0_hi")[:])
         for t in range(1, PACK):
             nc.vector.tensor_copy(out=a_t[t][:, 0:J], in_=first_stage(t, slice(0, J), f"acc{t}")[:])
 
-        x3_s = keep.tile([P, O], U8, name="x3_s", align_bytes=64)
-        x3_w = keep.tile([P, O], U16, name="x3_w", align_bytes=64)
+        x3_s = keep.tile([P, O], U8, name="x3_s", tag="x1_s", align_bytes=64)
         nc.vector.tensor_copy(x3_s[:], xt_s[:].indirect(list3[:]))
+        x3_w = keep.tile([P, O], U16, name="x3_w", tag="x1_w", align_bytes=64)
         nc.vector.tensor_copy(x3_w[:], xt_w[:].indirect(list3[:]))
-        late_p = keep.tile([P, 2 * N], U8, name="late_p", tag="w_wp1", align_bytes=64)
-        for h in range(2):
-            nc.vector.tensor_copy(
-                out=late_p[64 * h : 64 * (h + 1), :].bitcast(I32), in_=late_s[64:128, h, :].bitcast(I32)
-            )
         hid = keep.tile([P, O, PACK], BF16, name="hid", align_bytes=64)
         hid_w = keep.tile([P, O], U32, name="hid_w", align_bytes=64)
         hid_s = keep.tile([P, O], U8, name="hid_s", align_bytes=64)
@@ -157,7 +144,7 @@ def tile_list_pooledpicks_solo_further_tabled_kernel(
             nc.tensor.matmul_mx(
                 out=res[b][:],
                 lhsT=ws_w[:, b * P : (b + 1) * P].bitcast(E4M3X4),
-                lhsT_scale=late_p[:, b * P : (b + 1) * P],
+                lhsT_scale=ws_s[:, b * P : (b + 1) * P],
                 rhs=x3_w[:].bitcast(E2M1X4),
                 rhs_scale=x3_s[:],
                 start=True,
@@ -184,7 +171,7 @@ def tile_list_pooledpicks_solo_further_tabled_kernel(
             nc.tensor.matmul_mx(
                 out=res[b][:],
                 lhsT=wb_w[:, 2 * b * P : 2 * (b + 1) * P].bitcast(E2M1X4),
-                lhsT_scale=late_p[:, N + b * P : N + (b + 1) * P],
+                lhsT_scale=wb_s[:, b * P : (b + 1) * P],
                 rhs=hid_w[:].bitcast(E5M2X4),
                 rhs_scale=hid_s[:],
                 start=False,

from contextlib import ExitStack

import concourse.mybir as mybir

K, T, J, R, I, O, N, E = 512, 1024, 256, 512, 256, 128, 256, 1024
FLOPS = 2 * K * R * J + 2 * R * N * O + 2 * K * N * O

F32 = mybir.dt.float32
BF16 = mybir.dt.bfloat16
I32 = mybir.dt.int32
U32 = mybir.dt.uint32
U16 = mybir.dt.uint16
U8 = mybir.dt.uint8
E4M3X4 = mybir.dt.float8_e4m3fn_x4
E5M2X4 = mybir.dt.float8_e5m2_x4
E2M1X4 = mybir.dt.float4_e2m1fn_x4
COPY = mybir.ActivationFunctionType.Copy
MAX = mybir.AluOpType.max
ADD = mybir.AluOpType.add

P = 128
PACK = 4
HALF = I // 2


def load_scale_rows(queue, plane, scales, q):
    queue.dma_start(
        out=plane[32 * q : 32 * q + 4, :].bitcast(I32), in_=scales[0].bitcast(I32)[4 * q : 4 * q + 4, :]
    )


def tile_list_pooledpicks_solo_further_tabled_kernel(
    tc, xt_words, xt_scales, w_words, w_scales, sa, wb_words, wb_scales, ws_words, ws_scales, tz,
    offs, offs2, offs3, offs4, out,
):
    nc = tc.nc
    with ExitStack() as ctx:
        keep = ctx.enter_context(tc.tile_pool(name="keep", bufs=1))
        psum = ctx.enter_context(tc.psum_pool(name="psum", bufs=1))

        list1 = keep.tile([P, J // 16], U16, name="list1")
        list2 = keep.tile([P, I // 16], U16, name="list2")
        list3 = keep.tile([P, O // 16], U16, name="list3")
        list4 = keep.tile([P, O // 16], U16, name="list4")
        xt_w = keep.tile([P, T], U16, name="xt_w", align_bytes=64)
        xt_s = keep.tile([P, T], U8, name="xt_s", align_bytes=64)
        w_w = keep.tile([P, R], U32, name="w_w", align_bytes=64)
        w_stage = keep.tile([4, 4, R // 4], I32, name="w_stage", align_bytes=64)
        w_s = keep.tile([P, R], U8, name="w_s", align_bytes=64)
        ws_s = keep.tile([P, N], U8, name="ws_s", align_bytes=64)
        wb_s = keep.tile([P, N], U8, name="wb_s", align_bytes=64)
        ws_w = keep.tile([P, N], U32, name="ws_w", align_bytes=64)
        wb_w = keep.tile([P, 2 * N], U8, name="wb_w", align_bytes=64)
        sa_t = keep.tile([P, PACK], F32, name="sa_t")
        tz_t = keep.tile([P, 2, E], F32, name="tz_t")

        nc.vector.memset(xt_s[:].bitcast(I32), 0)
        nc.vector.memset(w_s[:].bitcast(I32), 0)

        w_s_words = w_s[:].bitcast(I32)
        nc.sync.dma_start(out=w_stage[:], in_=w_scales[0].bitcast(I32).rearrange("(q r) c -> r q c", q=4))
        nc.sync.dma_start(out=xt_w[:].bitcast(I32), in_=xt_words[0].bitcast(I32))
        nc.sync.dma_start(list1[:], offs)
        nc.sync.dma_start(out=w_w[:].bitcast(I32), in_=w_words[0].rearrange("p n t -> p (n t)").bitcast(I32))
        for q in range(4):
            load_scale_rows(nc.sync, xt_s, xt_scales, q)
        nc.sync.dma_start(list2[:], offs2)
        nc.sync.dma_start(out=sa_t[:], in_=sa.rearrange("(p t) o -> p (t o)", t=PACK))
        nc.sync.dma_start(list3[:], offs3)
        nc.sync.dma_start(list4[:], offs4)
        for q in range(3):
            load_scale_rows(nc.sync, ws_s, ws_scales, q)
        nc.sync.dma_start(out=tz_t[:], in_=tz.rearrange("(b p) e -> p b e", p=P))
        load_scale_rows(nc.sync, ws_s, ws_scales, 3)
        nc.sync.dma_start(out=ws_w[:].bitcast(I32), in_=ws_words[0].rearrange("p n t -> p (n t)").bitcast(I32))
        nc.sync.dma_start(out=wb_w[:].bitcast(I32), in_=wb_words[0].bitcast(I32))
        for q in range(4):
            load_scale_rows(nc.sync, wb_s, wb_scales, q)

        for q in range(4):
            nc.vector.tensor_copy(out=w_s_words[32 * q : 32 * q + 4, :], in_=w_stage[:, q, :])
        w_s_by_t = w_s[:].rearrange("p (m t) -> p t m", t=PACK)
        w_sp = keep.tile([P, PACK, P], U8, name="w_sp", align_bytes=64)
        nc.vector.tensor_copy(out=w_sp[:], in_=w_s_by_t)
        w_wp = [keep.tile([P, 2, P], U32, name=f"w_wp{u}", align_bytes=64) for u in range(2)]
        w_by_t = w_w[:].rearrange("p (c i t) -> p c t i", i=4, t=PACK)
        for u in range(2):
            nc.scalar.copy(
                out=w_wp[u][:].rearrange("p t (c i) -> p c t i", i=4), in_=w_by_t[:, :, 2 * u : 2 * u + 2, :]
            )

        x1_s = keep.tile([P, J], U8, name="x1_s", align_bytes=64)
        x1_w = keep.tile([P, J], U16, name="x1_w", align_bytes=64)
        nc.vector.tensor_copy(x1_w[:], xt_w[:].indirect(list1[:]))
        for h in range(2):
            nc.vector.tensor_copy(x1_s[:, h * P : (h + 1) * P], xt_s[:].indirect(list1[:, 8 * h : 8 * h + 8]))

        def first_stage(t, cols, name):
            acc = psum.tile([P, cols.stop - cols.start], F32, name=name)
            nc.tensor.matmul_mx(
                out=acc[:],
                lhsT=w_wp[t // 2][:, t % 2, :].bitcast(E4M3X4),
                lhsT_scale=w_sp[:, t, :],
                rhs=x1_w[:, cols].bitcast(E2M1X4),
                rhs_scale=x1_s[:, cols],
                start=True,
                stop=True,
            )
            return acc

        a_t = [keep.tile([P, 2 * J if t < 2 else J], F32, name=f"a{t}") for t in range(PACK)]
        nc.scalar.copy(out=a_t[0][:, 0:P], in_=first_stage(0, slice(0, P), "acc0_lo")[:])
        nc.scalar.copy(out=a_t[0][:, P:J], in_=first_stage(0, slice(P, J), "acc0_hi")[:])
        for t in range(1, PACK):
            nc.vector.tensor_copy(out=a_t[t][:, 0:J], in_=first_stage(t, slice(0, J), f"acc{t}")[:])

        x3_s = keep.tile([P, O], U8, name="x3_s", tag="x1_s", align_bytes=64)
        nc.vector.tensor_copy(x3_s[:], xt_s[:].indirect(list3[:]))
        x3_w = keep.tile([P, O], U16, name="x3_w", tag="x1_w", align_bytes=64)
        nc.vector.tensor_copy(x3_w[:], xt_w[:].indirect(list3[:]))
        hid = keep.tile([P, O, PACK], BF16, name="hid", align_bytes=64)
        hid_w = keep.tile([P, O], U32, name="hid_w", align_bytes=64)
        hid_s = keep.tile([P, O], U8, name="hid_s", align_bytes=64)

        def pick(dst, t, cols):
            nc.scalar.activation(
                out=dst,
                in_=a_t[t][:].indirect(list2[:, cols]),
                func=COPY,
                scale=sa_t[:, t : t + 1],
            )

        def pool_pairs(picks, pools, t0):
            pairs = picks.rearrange("p (t o e) -> p e o t", t=2, e=2)
            nc.vector.tensor_tensor(out=hid[:, pools, t0 : t0 + 2], in0=pairs[:, 0], in1=pairs[:, 1], op=MAX)

        h1_lo = keep.tile([P, 2 * I], F32, name="h1_lo")
        for t in range(2):
            pick(h1_lo[:, t * I : (t + 1) * I], t, slice(0, 16))
        pool_pairs(h1_lo[:], slice(0, O), 0)

        res = [psum.tile([P, O], F32, name=f"res{b}") for b in range(2)]
        for b in range(2):
            nc.tensor.matmul_mx(
                out=res[b][:],
                lhsT=ws_w[:, b * P : (b + 1) * P].bitcast(E4M3X4),
                lhsT_scale=ws_s[:, b * P : (b + 1) * P],
                rhs=x3_w[:].bitcast(E2M1X4),
                rhs_scale=x3_s[:],
                start=True,
                stop=False,
            )

        for h in range(2):
            h1_hi = keep.tile([P, 2 * HALF], F32, name=f"h1_hi{h}")
            for t in range(2, 4):
                pick(h1_hi[:, (t - 2) * HALF : (t - 1) * HALF], t, slice(8 * h, 8 * h + 8))
            pools = slice(h * O // 2, (h + 1) * O // 2)
            pool_pairs(h1_hi[:], pools, 2)
            nc.vector.quantize_mx(
                out=hid_w[:, pools].bitcast(E5M2X4),
                scales=hid_s[:, pools],
                in_=hid[:, pools, :].rearrange("p o t -> p (o t)"),
            )

        tz_g = keep.tile([P, 2, O], F32, name="tz_g", tag="a3")
        for b in range(2):
            nc.scalar.activation(out=tz_g[:, b, :], in_=tz_t[:, b, :].indirect(list4[:]), func=COPY)

        for b in range(2):
            nc.tensor.matmul_mx(
                out=res[b][:],
                lhsT=wb_w[:, 2 * b * P : 2 * (b + 1) * P].bitcast(E2M1X4),
                lhsT_scale=wb_s[:, b * P : (b + 1) * P],
                rhs=hid_w[:].bitcast(E5M2X4),
                rhs_scale=hid_s[:],
                start=False,
                stop=True,
            )
            y = keep.tile([P, O], F32, name=f"y{b}")
            nc.vector.tensor_tensor(out=y[:], in0=res[b][:], in1=tz_g[:, b, :], op=ADD)
            (nc.sync if b == 0 else nc.scalar).dma_start(out=out[b * P : (b + 1) * P, :], in_=y[:])
